import numpy as np
import ml_dtypes


def mxq(x, axis, fmt="e4m3"):
    dtype, down = {"e4m3": (ml_dtypes.float8_e4m3fn, 7), "e5m2": (ml_dtypes.float8_e5m2, 14)}[fmt]
    v = np.moveaxis(np.asarray(x, np.float32).astype(ml_dtypes.bfloat16).astype(np.float64), axis, -1)
    blocks = v.reshape(v.shape[:-1] + (-1, 32))
    amax = np.abs(blocks).max(-1, keepdims=True)
    byte = np.maximum(np.where(amax > 0, np.frexp(amax)[1] - 1 + 127, 0) - down, 1)
    scale = np.exp2(byte - 127.0)
    codes = (blocks / scale).astype(np.float32).astype(dtype).astype(np.float64)
    return np.moveaxis((codes * scale).reshape(v.shape), -1, axis)


WIDE = False


def mx_kscale(k, group=512):
    if not WIDE:
        return np.ones(k)
    levels = np.array([10, -10, 5, -5, 0])
    if group != 512:
        return np.exp2(np.random.permutation(np.resize(levels, k // group))).repeat(group)
    if k % 512:
        return np.exp2(np.random.permutation(np.resize(levels, k // 32))).repeat(32)
    a = np.empty((k // 512, 16))
    for p in range(k // 512):
        a[p, :8] = np.random.permutation(np.resize(levels, 8))
        for g in range(8):
            far = levels[np.abs(levels - a[p, g]) >= 10]
            a[p, g + 8] = far[np.random.randint(len(far))]
    return np.exp2(a.ravel()).repeat(32)


def f64(x):
    return np.asarray(x).astype(np.float64)


def silu(v):
    return v / (1.0 + np.exp(-v))


G, D, M, N = 4, 256, 128, 1024


def setup_inputs():
    n = np.random.standard_normal
    s = mx_kscale(D, 0)[:, None]
    return {
        "x": (n((G, D, N)) * s).astype(np.float32),
        "w": (n((G, D, M)) / np.sqrt(D) / s).astype(np.float32),
        "u": (n((G, D, M)) / np.sqrt(D) / s).astype(np.float32),
        "b": (0.5 * n((G, M, 1))).astype(np.float32),
        "r": n((G, M, N)).astype(np.float32),
    }


def reference(x, w, u, b, r):
    xq = mxq(f64(x), 1, "e4m3")
    h = mxq(f64(w), 1, "e4m3").transpose(0, 2, 1) @ xq
    g = mxq(f64(u), 1, "e4m3").transpose(0, 2, 1) @ xq
    h = h + f64(b)
    y = silu(h) * g
    y = y + f64(r)
    return y

@@ -1,0 +1,115 @@
+from contextlib import ExitStack
+
+import concourse.mybir as mybir
+
+G, D, M, N = 4, 256, 128, 1024
+FLOPS = 2 * 2 * G * D * M * N
+
+F32 = mybir.dt.float32
+BF16 = mybir.dt.bfloat16
+U32 = mybir.dt.uint32
+U8 = mybir.dt.uint8
+FP8X4 = mybir.dt.float8_e4m3fn_x4
+ACT = mybir.ActivationFunctionType
+
+P = 128
+PACK = 4
+ROWS = D // PACK
+CHUNK = 512
+LOADS = ["x0","w0","w1","x1","x2","w2","w3","r0","x3","r1","r2","r3"]
+VECTOR_COLS = [320,320,192,128]
+STEPS = ["xv0","xa0","wv0","xq0","wa1","wq0","mm00","wq1","mm01","xv1","xa1","si00","si01","xq1","mu00","mu01","mm10","mm11","xv2","xa2","wv2","wa3","xq2","wq2","wq3","si10","si11","ad00","ad01","st0","mu10","mu11","mm20","mm21","si20","xa3","mu20","xv3","ad10","xq3","mm30","mm31","si21","ad11","st1","mu21","ad20","st20","si30","si31","ad21","st21","mu30","mu31","ad30","st30","ad31","st31"]
+
+
+def interleave(copy, dst, src, c0, c1):
+    copy(
+        out=dst[:, c0:c1, :].rearrange("p (c i) t -> p c t i", i=4),
+        in_=src[:, :, c0:c1].rearrange("p t (c i) -> p c t i", i=4),
+    )
+
+
+def tile_rows_gglu_silu_bias_res_kernel(tc, x, w, u, b, r, out):
+    nc = tc.nc
+    with ExitStack() as ctx:
+        sb = ctx.enter_context(tc.tile_pool(name="sb", bufs=1))
+        ps = ctx.enter_context(tc.psum_pool(name="ps", bufs=1))
+        ctx.enter_context(tc.manual_schedule())
+
+        def tiles(name, count, shape, dtype):
+            return [sb.tile(shape, dtype, name="%s%d" % (name, i), align_bytes=64) for i in range(count)]
+
+        x_raw = tiles("x_raw", 4, [P, PACK, CHUNK], F32)
+        x_bf = tiles("x_bf", 4, [P, CHUNK, PACK], BF16)
+        x_codes = tiles("x_codes", 4, [P, CHUNK], U32)
+        x_scales = tiles("x_scales", 4, [P, CHUNK], U8)
+        w_raw = tiles("w_raw", 4, [P, PACK, M], F32)
+        w_bf = tiles("w_bf", 4, [P, M, PACK], BF16)
+        w_codes = tiles("w_codes", 4, [P, M], U32)
+        w_scales = tiles("w_scales", 4, [P, M], U8)
+        res = tiles("res", 4, [P, 2, CHUNK], F32)
+        gate = tiles("gate", 4, [P, 2, CHUNK], F32)
+        prod = tiles("prod", 4, [P, 2, CHUNK], F32)
+        y = tiles("y", 4, [P, 2, CHUNK], F32)
+        bias = sb.tile([P, G, 8], F32, name="bias")
+        warm = sb.tile([P, 8], F32, name="warm")
+        banks = [[[ps.tile([M, CHUNK], F32, name="acc%d%d%d" % (s, c, v)) for v in range(2)] for c in range(2)] for s in range(2)]
+
+        def view(t, k):
+            a, hf = divmod(k, 2)
+            return t[2 * a : 2 * a + 2, :, hf * CHUNK : (hf + 1) * CHUNK]
+
+        with nc.allow_non_contiguous_dma(reason="one bias value to a partition"):
+            nc.scalar.dma_start(out=bias[:, :, 0:1], in_=b.rearrange("g m o -> m g o"))
+        nc.vector.memset(warm[:, 0:1], 0.0)
+        nc.scalar.activation(out=warm[:, 4:5], in_=warm[:, 0:1], func=ACT.Silu)
+
+        for name in LOADS:
+            k = int(name[1])
+            if name[0] == "x":
+                nc.sync.dma_start(out=x_raw[k][:], in_=view(x, k).rearrange("g (p j) n -> (g p) j n", j=PACK))
+            elif name[0] == "r":
+                nc.sync.dma_start(out=res[k][:], in_=view(r, k).rearrange("g m n -> m g n"))
+            else:
+                a, v = divmod(k, 2)
+                nc.sync.dma_start(out=w_raw[k][:], in_=(w, u)[v][2 * a : 2 * a + 2].rearrange("g (p j) m -> (g p) j m", j=PACK))
+
+        for name in STEPS:
+            kind, k = name[:2], int(name[2])
+            c = int(name[3]) if len(name) > 3 else None
+            if kind == "xv":
+                interleave(nc.vector.tensor_copy, x_bf[k], x_raw[k], 0, VECTOR_COLS[k])
+            elif kind == "xa":
+                interleave(nc.scalar.copy, x_bf[k], x_raw[k], VECTOR_COLS[k], CHUNK)
+            elif kind == "wv":
+                interleave(nc.vector.tensor_copy, w_bf[k], w_raw[k], 0, M)
+            elif kind == "wa":
+                interleave(nc.scalar.copy, w_bf[k], w_raw[k], 0, M)
+            elif kind == "xq":
+                nc.vector.quantize_mx(out=x_codes[k][:].bitcast(FP8X4), scales=x_scales[k][:], in_=x_bf[k][:].rearrange("p n j -> p (n j)"))
+            elif kind == "wq":
+                nc.vector.quantize_mx(out=w_codes[k][:].bitcast(FP8X4), scales=w_scales[k][:], in_=w_bf[k][:].rearrange("p n j -> p (n j)"))
+            elif kind == "mm":
+                wk = 2 * (k // 2) + c
+                for cc in range(2):
+                    rows = slice(ROWS * cc, ROWS * (cc + 1))
+                    nc.tensor.matmul_mx(
+                        out=banks[k % 2][cc][c][:],
+                        lhsT=w_codes[wk][rows, :].bitcast(FP8X4),
+                        lhsT_scale=w_scales[wk][rows, :],
+                        rhs=x_codes[k][rows, :].bitcast(FP8X4),
+                        rhs_scale=x_scales[k][rows, :],
+                        start=True,
+                        stop=True,
+                    )
+            elif kind == "si":
+                g = 2 * (k // 2) + c
+                nc.scalar.activation(out=gate[k][:, c, :], in_=banks[k % 2][c][0][:], func=ACT.Silu, bias=bias[:, g, 0:1])
+            elif kind == "mu":
+                nc.vector.tensor_mul(out=prod[k][:, c, :], in0=banks[k % 2][c][1][:], in1=gate[k][:, c, :])
+            elif kind == "ad":
+                nc.vector.tensor_add(out=y[k][:, c, :], in0=prod[k][:, c, :], in1=res[k][:, c, :])
+            elif kind == "st":
+                if c is None:
+                    nc.sync.dma_start(out=view(out, k).rearrange("g m n -> m g n"), in_=y[k][:])
+                else:
+                    nc.sync.dma_start(out=view(out, k)[c], in_=y[k][:, c, :])

@@ -16,9 +16,13 @@ P = 128
 PACK = 4
 ROWS = D // PACK
 CHUNK = 512
-LOADS = ["x0","w0","w1","x1","x2","w2","w3","r0","x3","r1","r2","r3"]
-VECTOR_COLS = [320,320,192,128]
-STEPS = ["xv0","xa0","wv0","xq0","wa1","wq0","mm00","wq1","mm01","xv1","xa1","si00","si01","xq1","mu00","mu01","mm10","mm11","xv2","xa2","wv2","wa3","xq2","wq2","wq3","si10","si11","ad00","ad01","st0","mu10","mu11","mm20","mm21","si20","xa3","mu20","xv3","ad10","xq3","mm30","mm31","si21","ad11","st1","mu21","ad20","st20","si30","si31","ad21","st21","mu30","mu31","ad30","st30","ad31","st31"]
+NMM = 128
+UNITS = [[0,0,512],[1,0,512],[2,0,512],[3,0,256],[3,256,256]]
+LOADS = ["x0","b0","w0","w1","x1","x2","w2","w3","r0","r1","x3","x4","r2","r3"]
+VECTOR_COLS = [448,256,448,0,0]
+W_ON_VECTOR = []
+ON_POOL = []
+STEPS = ["V0","A0","T0","W0","q0","W1","Q0","h00","Q1","s00","h01","V1","A1","g00","m00","s01","g01","q1","A2","h10","m01","W2","h11","V2","W3","g10","Q2","s10","g11","q2","s11","h20","Q3","s20","h21","a00","s21","g20","a01","A3","g21","o0","m10","A4","m11","a10","a11","o1","m20","q3","h30","m21","s30","h31","a20","s31","g30","q4","g31","a21","h40","o2","m30","s40","h41","m31","s41","g40","a30","g41","a31","o3","m40","m41","a40","a41","o4"]
 
 
 def interleave(copy, dst, src, c0, c1):
@@ -35,81 +39,93 @@ def tile_rows_gglu_silu_bias_res_kernel(tc, x, w, u, b, r, out):
         ps = ctx.enter_context(tc.psum_pool(name="ps", bufs=1))
         ctx.enter_context(tc.manual_schedule())
 
-        def tiles(name, count, shape, dtype):
-            return [sb.tile(shape, dtype, name="%s%d" % (name, i), align_bytes=64) for i in range(count)]
+        def tiles(name, shapes, dtype):
+            return [sb.tile(shape, dtype, name="%s%d" % (name, i), align_bytes=64) for i, shape in enumerate(shapes)]
 
-        x_raw = tiles("x_raw", 4, [P, PACK, CHUNK], F32)
-        x_bf = tiles("x_bf", 4, [P, CHUNK, PACK], BF16)
-        x_codes = tiles("x_codes", 4, [P, CHUNK], U32)
-        x_scales = tiles("x_scales", 4, [P, CHUNK], U8)
-        w_raw = tiles("w_raw", 4, [P, PACK, M], F32)
-        w_bf = tiles("w_bf", 4, [P, M, PACK], BF16)
-        w_codes = tiles("w_codes", 4, [P, M], U32)
-        w_scales = tiles("w_scales", 4, [P, M], U8)
-        res = tiles("res", 4, [P, 2, CHUNK], F32)
-        gate = tiles("gate", 4, [P, 2, CHUNK], F32)
-        prod = tiles("prod", 4, [P, 2, CHUNK], F32)
-        y = tiles("y", 4, [P, 2, CHUNK], F32)
-        bias = sb.tile([P, G, 8], F32, name="bias")
+        widths = [unit[2] for unit in UNITS]
+        x_raw = tiles("x_raw", [[P, PACK, n] for n in widths], F32)
+        x_bf = tiles("x_bf", [[P, n, PACK] for n in widths], BF16)
+        x_codes = tiles("x_codes", [[P, n] for n in widths], U32)
+        x_scales = tiles("x_scales", [[P, n] for n in widths], U8)
+        w_raw = tiles("w_raw", [[P, PACK, M]] * 4, F32)
+        w_bf = tiles("w_bf", [[P, M, PACK]] * 4, BF16)
+        w_codes = tiles("w_codes", [[P, M]] * 4, U32)
+        w_scales = tiles("w_scales", [[P, M]] * 4, U8)
+        res = tiles("res", [[P, 2, CHUNK]] * 4, F32)
+        gate = tiles("gate", [[P, 2, n] for n in widths], F32)
+        prod = tiles("prod", [[P, 2, n] for n in widths], F32)
+        y = tiles("y", [[P, 2, n] for n in widths], F32)
+        bias_rows = sb.tile([P, G * 32], F32, name="bias_rows", align_bytes=64)
+        bias = sb.tile([P, G * 32], F32, name="bias", align_bytes=64)
         warm = sb.tile([P, 8], F32, name="warm")
         banks = [[[ps.tile([M, CHUNK], F32, name="acc%d%d%d" % (s, c, v)) for v in range(2)] for c in range(2)] for s in range(2)]
 
-        def view(t, k):
+        def view(t, k, c0, n):
             a, hf = divmod(k, 2)
-            return t[2 * a : 2 * a + 2, :, hf * CHUNK : (hf + 1) * CHUNK]
+            return t[2 * a : 2 * a + 2, :, hf * CHUNK + c0 : hf * CHUNK + c0 + n]
 
-        with nc.allow_non_contiguous_dma(reason="one bias value to a partition"):
-            nc.scalar.dma_start(out=bias[:, :, 0:1], in_=b.rearrange("g m o -> m g o"))
+        nc.vector.memset(bias_rows[:], 0.0)
         nc.vector.memset(warm[:, 0:1], 0.0)
         nc.scalar.activation(out=warm[:, 4:5], in_=warm[:, 0:1], func=ACT.Silu)
 
         for name in LOADS:
             k = int(name[1])
             if name[0] == "x":
-                nc.sync.dma_start(out=x_raw[k][:], in_=view(x, k).rearrange("g (p j) n -> (g p) j n", j=PACK))
+                nc.sync.dma_start(out=x_raw[k][:], in_=view(x, *UNITS[k]).rearrange("g (p j) n -> (g p) j n", j=PACK))
+            elif name[0] == "b":
+                nc.sync.dma_start(
+                    out=bias_rows[0:P:32, :].rearrange("q (g j) -> q g j", g=G),
+                    in_=b.rearrange("g (q j) o -> q g (j o)", j=32),
+                )
             elif name[0] == "r":
-                nc.sync.dma_start(out=res[k][:], in_=view(r, k).rearrange("g m n -> m g n"))
+                nc.sync.dma_start(out=res[k][:], in_=view(r, k, 0, CHUNK).rearrange("g m n -> m g n"))
             else:
                 a, v = divmod(k, 2)
                 nc.sync.dma_start(out=w_raw[k][:], in_=(w, u)[v][2 * a : 2 * a + 2].rearrange("g (p j) m -> (g p) j m", j=PACK))
 
         for name in STEPS:
-            kind, k = name[:2], int(name[2])
-            c = int(name[3]) if len(name) > 3 else None
-            if kind == "xv":
-                interleave(nc.vector.tensor_copy, x_bf[k], x_raw[k], 0, VECTOR_COLS[k])
-            elif kind == "xa":
-                interleave(nc.scalar.copy, x_bf[k], x_raw[k], VECTOR_COLS[k], CHUNK)
-            elif kind == "wv":
-                interleave(nc.vector.tensor_copy, w_bf[k], w_raw[k], 0, M)
-            elif kind == "wa":
-                interleave(nc.scalar.copy, w_bf[k], w_raw[k], 0, M)
-            elif kind == "xq":
-                nc.vector.quantize_mx(out=x_codes[k][:].bitcast(FP8X4), scales=x_scales[k][:], in_=x_bf[k][:].rearrange("p n j -> p (n j)"))
-            elif kind == "wq":
+            kind, k = name[0], int(name[1])
+            c = int(name[2]) if len(name) > 2 else None
+            if kind == "T":
+                nc.vector.transpose(out=bias[:], in_=bias_rows[:])
+                continue
+            if kind == "W":
+                interleave(nc.vector.tensor_copy if k in W_ON_VECTOR else nc.scalar.copy, w_bf[k], w_raw[k], 0, M)
+                continue
+            if kind == "Q":
                 nc.vector.quantize_mx(out=w_codes[k][:].bitcast(FP8X4), scales=w_scales[k][:], in_=w_bf[k][:].rearrange("p n j -> p (n j)"))
-            elif kind == "mm":
-                wk = 2 * (k // 2) + c
-                for cc in range(2):
-                    rows = slice(ROWS * cc, ROWS * (cc + 1))
-                    nc.tensor.matmul_mx(
-                        out=banks[k % 2][cc][c][:],
-                        lhsT=w_codes[wk][rows, :].bitcast(FP8X4),
-                        lhsT_scale=w_scales[wk][rows, :],
-                        rhs=x_codes[k][rows, :].bitcast(FP8X4),
-                        rhs_scale=x_scales[k][rows, :],
-                        start=True,
-                        stop=True,
-                    )
-            elif kind == "si":
-                g = 2 * (k // 2) + c
-                nc.scalar.activation(out=gate[k][:, c, :], in_=banks[k % 2][c][0][:], func=ACT.Silu, bias=bias[:, g, 0:1])
-            elif kind == "mu":
-                nc.vector.tensor_mul(out=prod[k][:, c, :], in0=banks[k % 2][c][1][:], in1=gate[k][:, c, :])
-            elif kind == "ad":
-                nc.vector.tensor_add(out=y[k][:, c, :], in0=prod[k][:, c, :], in1=res[k][:, c, :])
-            elif kind == "st":
-                if c is None:
-                    nc.sync.dma_start(out=view(out, k).rearrange("g m n -> m g n"), in_=y[k][:])
-                else:
-                    nc.sync.dma_start(out=view(out, k)[c], in_=y[k][:, c, :])
+                continue
+            chunk, c0, n = UNITS[k]
+            if kind == "V":
+                interleave(nc.vector.tensor_copy, x_bf[k], x_raw[k], 0, VECTOR_COLS[k])
+            elif kind == "A":
+                interleave(nc.scalar.copy, x_bf[k], x_raw[k], VECTOR_COLS[k], n)
+            elif kind == "q":
+                nc.vector.quantize_mx(out=x_codes[k][:].bitcast(FP8X4), scales=x_scales[k][:], in_=x_bf[k][:].rearrange("p n j -> p (n j)"))
+            elif kind == "h" or kind == "g":
+                v = 0 if kind == "h" else 1
+                wk = 2 * (chunk // 2) + v
+                for cc in (c,):
+                    for j in range(0, n, NMM):
+                        rows = slice(ROWS * cc, ROWS * (cc + 1))
+                        nc.tensor.matmul_mx(
+                            out=banks[k % 2][cc][v][:, j : j + NMM],
+                            lhsT=w_codes[wk][rows, :].bitcast(FP8X4),
+                            lhsT_scale=w_scales[wk][rows, :],
+                            rhs=x_codes[k][rows, j : j + NMM].bitcast(FP8X4),
+                            rhs_scale=x_scales[k][rows, j : j + NMM],
+                            start=True,
+                            stop=True,
+                        )
+            elif kind == "s":
+                g = 2 * (chunk // 2) + c
+                nc.scalar.activation(out=gate[k][:, c, :], in_=banks[k % 2][c][0][:, 0:n], func=ACT.Silu, bias=bias[:, 32 * g : 32 * g + 1])
+            elif kind == "m":
+                nc.vector.tensor_mul(out=prod[k][:, c, :], in0=banks[k % 2][c][1][:, 0:n], in1=gate[k][:, c, :])
+            elif kind == "a":
+                eng = nc.gpsimd if name in ON_POOL else nc.vector
+                eng.tensor_add(out=y[k][:, c, :], in0=prod[k][:, c, :], in1=res[chunk][:, c, c0 : c0 + n])
+            elif c is None:
+                nc.sync.dma_start(out=view(out, chunk, c0, n).rearrange("g m n -> m g n"), in_=y[k][:])
+            else:
+                nc.sync.dma_start(out=view(out, chunk, c0, n)[c], in_=y[k][:, c, :])

@@ -18,11 +18,11 @@ ROWS = D // PACK
 CHUNK = 512
 NMM = 128
 UNITS = [[0,0,512],[1,0,512],[2,0,512],[3,0,256],[3,256,256]]
-LOADS = ["x0","b0","w0","w1","x1","x2","w2","w3","r0","r1","x3","x4","r2","r3"]
-VECTOR_COLS = [448,256,448,0,0]
+LOADS = ["x0","b0","w0","w1","w2","x2","w3","r0","x3","r1","r2","r3"]
+VECTOR_COLS = [384,384,256,0,0]
 W_ON_VECTOR = []
 ON_POOL = []
-STEPS = ["V0","A0","T0","W0","q0","W1","Q0","h00","Q1","s00","h01","V1","A1","g00","m00","s01","g01","q1","A2","h10","m01","W2","h11","V2","W3","g10","Q2","s10","g11","q2","s11","h20","Q3","s20","h21","a00","s21","g20","a01","A3","g21","o0","m10","A4","m11","a10","a11","o1","m20","q3","h30","m21","s30","h31","a20","s31","g30","q4","g31","a21","h40","o2","m30","s40","h41","m31","s41","g40","a30","g41","a31","o3","m40","m41","a40","a41","o4"]
+STEPS = ["V0","A0","T0","W0","q0","W1","Q0","W2","h00","Q1","A1","h01","V1","s00","g00","Q2","s01","g01","q1","A2","h10","m00","W3","h11","V2","s10","g10","m01","s11","g11","q2","h20","a00","s20","h21","Q3","s21","g20","m10","A3","g21","m11","A4","a10","o0","m20","m21","a11","a01","o1","q3","h30","a20","s30","h31","q4","s31","g30","a21","g31","o2","m30","h40","m31","s40","h41","a30","s41","g40","a31","g41","o3","m40","m41","a40","a41","o4"]
 
 
 def interleave(copy, dst, src, c0, c1):
@@ -43,7 +43,9 @@ def tile_rows_gglu_silu_bias_res_kernel(tc, x, w, u, b, r, out):
             return [sb.tile(shape, dtype, name="%s%d" % (name, i), align_bytes=64) for i, shape in enumerate(shapes)]
 
         widths = [unit[2] for unit in UNITS]
-        x_raw = tiles("x_raw", [[P, PACK, n] for n in widths], F32)
+        x_pair = sb.tile([P, PACK, N], F32, name="x_pair", align_bytes=64)
+        x_half = tiles("x_half", [[P, PACK, CHUNK]] * 2, F32)
+        x_raw = [x_pair[:, :, 0:512], x_pair[:, :, 512:1024], x_half[0][:], x_half[1][:, :, 0:256], x_half[1][:, :, 256:512]]
         x_bf = tiles("x_bf", [[P, n, PACK] for n in widths], BF16)
         x_codes = tiles("x_codes", [[P, n] for n in widths], U32)
         x_scales = tiles("x_scales", [[P, n] for n in widths], U8)
@@ -71,14 +73,20 @@ def tile_rows_gglu_silu_bias_res_kernel(tc, x, w, u, b, r, out):
         for name in LOADS:
             k = int(name[1])
             if name[0] == "x":
-                nc.sync.dma_start(out=x_raw[k][:], in_=view(x, *UNITS[k]).rearrange("g (p j) n -> (g p) j n", j=PACK))
+                if k == 0:
+                    nc.sync.dma_start(out=x_pair[:], in_=x[0:2].rearrange("g (p j) n -> (g p) j n", j=PACK))
+                else:
+                    nc.sync.dma_start(out=x_half[k - 2][:], in_=view(x, k, 0, CHUNK).rearrange("g (p j) n -> (g p) j n", j=PACK))
             elif name[0] == "b":
                 nc.sync.dma_start(
                     out=bias_rows[0:P:32, :].rearrange("q (g j) -> q g j", g=G),
                     in_=b.rearrange("g (q j) o -> q g (j o)", j=32),
                 )
             elif name[0] == "r":
-                nc.sync.dma_start(out=res[k][:], in_=view(r, k, 0, CHUNK).rearrange("g m n -> m g n"))
+                if k < 2:
+                    nc.sync.dma_start(out=res[k][:].rearrange("m h n -> m (h n)"), in_=r[k])
+                else:
+                    nc.sync.dma_start(out=res[k][:], in_=view(r, k, 0, CHUNK).rearrange("g m n -> m g n"))
             else:
                 a, v = divmod(k, 2)
                 nc.sync.dma_start(out=w_raw[k][:], in_=(w, u)[v][2 * a : 2 * a + 2].rearrange("g (p j) m -> (g p) j m", j=PACK))
@@ -124,7 +132,12 @@ def tile_rows_gglu_silu_bias_res_kernel(tc, x, w, u, b, r, out):
                 nc.vector.tensor_mul(out=prod[k][:, c, :], in0=banks[k % 2][c][1][:, 0:n], in1=gate[k][:, c, :])
             elif kind == "a":
                 eng = nc.gpsimd if name in ON_POOL else nc.vector
-                eng.tensor_add(out=y[k][:, c, :], in0=prod[k][:, c, :], in1=res[chunk][:, c, c0 : c0 + n])
+                if k < 2:
+                    eng.tensor_add(out=y[c][:, k, :], in0=prod[k][:, c, :], in1=res[c][:, k, :])
+                else:
+                    eng.tensor_add(out=y[k][:, c, :], in0=prod[k][:, c, :], in1=res[chunk][:, c, c0 : c0 + n])
+            elif k < 2:
+                nc.sync.dma_start(out=out[k], in_=y[k][:].rearrange("m h n -> m (h n)"))
             elif c is None:
                 nc.sync.dma_start(out=view(out, chunk, c0, n).rearrange("g m n -> m g n"), in_=y[k][:])
             else:

from contextlib import ExitStack

import concourse.mybir as mybir

G, D, M, N = 4, 256, 128, 1024
FLOPS = 2 * 2 * G * D * M * N

F32 = mybir.dt.float32
BF16 = mybir.dt.bfloat16
U32 = mybir.dt.uint32
U8 = mybir.dt.uint8
FP8X4 = mybir.dt.float8_e4m3fn_x4
ACT = mybir.ActivationFunctionType

P = 128
PACK = 4
ROWS = D // PACK
CHUNK = 512
NMM = 128
UNITS = [[0,0,512],[1,0,512],[2,0,512],[3,0,256],[3,256,256]]
LOADS = ["x0","b0","w0","w1","w2","x2","w3","r0","x3","r1","r2","r3"]
VECTOR_COLS = [384,384,256,0,0]
W_ON_VECTOR = []
ON_POOL = []
STEPS = ["V0","A0","T0","W0","q0","W1","Q0","W2","h00","Q1","A1","h01","V1","s00","g00","Q2","s01","g01","q1","A2","h10","m00","W3","h11","V2","s10","g10","m01","s11","g11","q2","h20","a00","s20","h21","Q3","s21","g20","m10","A3","g21","m11","A4","a10","o0","m20","m21","a11","a01","o1","q3","h30","a20","s30","h31","q4","s31","g30","a21","g31","o2","m30","h40","m31","s40","h41","a30","s41","g40","a31","g41","o3","m40","m41","a40","a41","o4"]


def interleave(copy, dst, src, c0, c1):
    copy(
        out=dst[:, c0:c1, :].rearrange("p (c i) t -> p c t i", i=4),
        in_=src[:, :, c0:c1].rearrange("p t (c i) -> p c t i", i=4),
    )


def tile_rows_gglu_silu_bias_res_kernel(tc, x, w, u, b, r, out):
    nc = tc.nc
    with ExitStack() as ctx:
        sb = ctx.enter_context(tc.tile_pool(name="sb", bufs=1))
        ps = ctx.enter_context(tc.psum_pool(name="ps", bufs=1))
        ctx.enter_context(tc.manual_schedule())

        def tiles(name, shapes, dtype):
            return [sb.tile(shape, dtype, name="%s%d" % (name, i), align_bytes=64) for i, shape in enumerate(shapes)]

        widths = [unit[2] for unit in UNITS]
        x_pair = sb.tile([P, PACK, N], F32, name="x_pair", align_bytes=64)
        x_half = tiles("x_half", [[P, PACK, CHUNK]] * 2, F32)
        x_raw = [x_pair[:, :, 0:512], x_pair[:, :, 512:1024], x_half[0][:], x_half[1][:, :, 0:256], x_half[1][:, :, 256:512]]
        x_bf = tiles("x_bf", [[P, n, PACK] for n in widths], BF16)
        x_codes = tiles("x_codes", [[P, n] for n in widths], U32)
        x_scales = tiles("x_scales", [[P, n] for n in widths], U8)
        w_raw = tiles("w_raw", [[P, PACK, M]] * 4, F32)
        w_bf = tiles("w_bf", [[P, M, PACK]] * 4, BF16)
        w_codes = tiles("w_codes", [[P, M]] * 4, U32)
        w_scales = tiles("w_scales", [[P, M]] * 4, U8)
        res = tiles("res", [[P, 2, CHUNK]] * 4, F32)
        gate = tiles("gate", [[P, 2, n] for n in widths], F32)
        prod = tiles("prod", [[P, 2, n] for n in widths], F32)
        y = tiles("y", [[P, 2, n] for n in widths], F32)
        bias_rows = sb.tile([P, G * 32], F32, name="bias_rows", align_bytes=64)
        bias = sb.tile([P, G * 32], F32, name="bias", align_bytes=64)
        warm = sb.tile([P, 8], F32, name="warm")
        banks = [[[ps.tile([M, CHUNK], F32, name="acc%d%d%d" % (s, c, v)) for v in range(2)] for c in range(2)] for s in range(2)]

        def view(t, k, c0, n):
            a, hf = divmod(k, 2)
            return t[2 * a : 2 * a + 2, :, hf * CHUNK + c0 : hf * CHUNK + c0 + n]

        nc.vector.memset(bias_rows[:], 0.0)
        nc.vector.memset(warm[:, 0:1], 0.0)
        nc.scalar.activation(out=warm[:, 4:5], in_=warm[:, 0:1], func=ACT.Silu)

        for name in LOADS:
            k = int(name[1])
            if name[0] == "x":
                if k == 0:
                    nc.sync.dma_start(out=x_pair[:], in_=x[0:2].rearrange("g (p j) n -> (g p) j n", j=PACK))
                else:
                    nc.sync.dma_start(out=x_half[k - 2][:], in_=view(x, k, 0, CHUNK).rearrange("g (p j) n -> (g p) j n", j=PACK))
            elif name[0] == "b":
                nc.sync.dma_start(
                    out=bias_rows[0:P:32, :].rearrange("q (g j) -> q g j", g=G),
                    in_=b.rearrange("g (q j) o -> q g (j o)", j=32),
                )
            elif name[0] == "r":
                if k < 2:
                    nc.sync.dma_start(out=res[k][:].rearrange("m h n -> m (h n)"), in_=r[k])
                else:
                    nc.sync.dma_start(out=res[k][:], in_=view(r, k, 0, CHUNK).rearrange("g m n -> m g n"))
            else:
                a, v = divmod(k, 2)
                nc.sync.dma_start(out=w_raw[k][:], in_=(w, u)[v][2 * a : 2 * a + 2].rearrange("g (p j) m -> (g p) j m", j=PACK))

        for name in STEPS:
            kind, k = name[0], int(name[1])
            c = int(name[2]) if len(name) > 2 else None
            if kind == "T":
                nc.vector.transpose(out=bias[:], in_=bias_rows[:])
                continue
            if kind == "W":
                interleave(nc.vector.tensor_copy if k in W_ON_VECTOR else nc.scalar.copy, w_bf[k], w_raw[k], 0, M)
                continue
            if kind == "Q":
                nc.vector.quantize_mx(out=w_codes[k][:].bitcast(FP8X4), scales=w_scales[k][:], in_=w_bf[k][:].rearrange("p n j -> p (n j)"))
                continue
            chunk, c0, n = UNITS[k]
            if kind == "V":
                interleave(nc.vector.tensor_copy, x_bf[k], x_raw[k], 0, VECTOR_COLS[k])
            elif kind == "A":
                interleave(nc.scalar.copy, x_bf[k], x_raw[k], VECTOR_COLS[k], n)
            elif kind == "q":
                nc.vector.quantize_mx(out=x_codes[k][:].bitcast(FP8X4), scales=x_scales[k][:], in_=x_bf[k][:].rearrange("p n j -> p (n j)"))
            elif kind == "h" or kind == "g":
                v = 0 if kind == "h" else 1
                wk = 2 * (chunk // 2) + v
                for cc in (c,):
                    for j in range(0, n, NMM):
                        rows = slice(ROWS * cc, ROWS * (cc + 1))
                        nc.tensor.matmul_mx(
                            out=banks[k % 2][cc][v][:, j : j + NMM],
                            lhsT=w_codes[wk][rows, :].bitcast(FP8X4),
                            lhsT_scale=w_scales[wk][rows, :],
                            rhs=x_codes[k][rows, j : j + NMM].bitcast(FP8X4),
                            rhs_scale=x_scales[k][rows, j : j + NMM],
                            start=True,
                            stop=True,
                        )
            elif kind == "s":
                g = 2 * (chunk // 2) + c
                nc.scalar.activation(out=gate[k][:, c, :], in_=banks[k % 2][c][0][:, 0:n], func=ACT.Silu, bias=bias[:, 32 * g : 32 * g + 1])
            elif kind == "m":
                nc.vector.tensor_mul(out=prod[k][:, c, :], in0=banks[k % 2][c][1][:, 0:n], in1=gate[k][:, c, :])
            elif kind == "a":
                eng = nc.gpsimd if name in ON_POOL else nc.vector
                if k < 2:
                    eng.tensor_add(out=y[c][:, k, :], in0=prod[k][:, c, :], in1=res[c][:, k, :])
                else:
                    eng.tensor_add(out=y[k][:, c, :], in0=prod[k][:, c, :], in1=res[chunk][:, c, c0 : c0 + n])
            elif k < 2:
                nc.sync.dma_start(out=out[k], in_=y[k][:].rearrange("m h n -> m (h n)"))
            elif c is None:
                nc.sync.dma_start(out=view(out, chunk, c0, n).rearrange("g m n -> m g n"), in_=y[k][:])
            else:
                nc.sync.dma_start(out=view(out, chunk, c0, n)[c], in_=y[k][:, c, :])
